import numpy as np
import ml_dtypes


def mxq(x, axis, fmt="e4m3"):
    dtype, down = {"e4m3": (ml_dtypes.float8_e4m3fn, 7), "e5m2": (ml_dtypes.float8_e5m2, 14)}[fmt]
    v = np.moveaxis(np.asarray(x, np.float32).astype(ml_dtypes.bfloat16).astype(np.float64), axis, -1)
    blocks = v.reshape(v.shape[:-1] + (-1, 32))
    amax = np.abs(blocks).max(-1, keepdims=True)
    byte = np.maximum(np.where(amax > 0, np.frexp(amax)[1] - 1 + 127, 0) - down, 1)
    scale = np.exp2(byte - 127.0)
    codes = (blocks / scale).astype(np.float32).astype(dtype).astype(np.float64)
    return np.moveaxis((codes * scale).reshape(v.shape), -1, axis)


WIDE = False


def mx_kscale(k):
    if not WIDE:
        return np.ones(k)
    levels = np.array([10, -10, 5, -5, 0])
    if k % 512:
        return np.exp2(np.random.permutation(np.resize(levels, k // 32))).repeat(32)
    a = np.empty((k // 512, 16))
    for p in range(k // 512):
        a[p, :8] = np.random.permutation(np.resize(levels, 8))
        for g in range(8):
            far = levels[np.abs(levels - a[p, g]) >= 10]
            a[p, g + 8] = far[np.random.randint(len(far))]
    return np.exp2(a.ravel()).repeat(32)


def f64(x):
    return np.asarray(x).astype(np.float64)


def striped(idx):
    return np.tile(idx.reshape(-1, 16).T, (8, 1)).astype(np.uint16)


def unstriped(offs):
    return offs[:16].T.reshape(-1).astype(np.int64)


def pack_weight(w):
    k, n = w.shape
    w = f64(np.asarray(w, np.float32).astype(ml_dtypes.bfloat16)).reshape(k // 32, 32, n)
    amax = np.abs(w).max(1)
    byte = np.clip(np.where(amax > 0, np.frexp(amax)[1] - 1 + 127 - 7, 1), 1, 254)
    scaled = (w * np.exp2(127.0 - byte)[:, None, :]).reshape(k, n).astype(np.float32)
    words = np.ascontiguousarray(scaled.reshape(k // 512, 128, 4, n).transpose(0, 1, 3, 2)).astype(ml_dtypes.float8_e4m3fn).view(np.uint8)
    return words, np.ascontiguousarray(byte.astype(np.uint8).reshape(k // 512, 16, n))


def unpack_weight(words, scales):
    g, p, n, _ = words.shape
    vals = np.ascontiguousarray(words).view(ml_dtypes.float8_e4m3fn).astype(np.float64) * np.repeat(np.exp2(scales.astype(np.float64) - 127.0), 8, axis=1)[..., None]
    return vals.transpose(0, 1, 3, 2).reshape(g * 512, n)


K, T, S, D, N, V = 512, 2048, 512, 2, 256, 256


def setup_inputs():
    n = np.random.standard_normal
    s = mx_kscale(K)[:, None]
    packed_xT = pack_weight(n((K, T)) * s)
    return {
        "x_words": packed_xT[0],
        "x_scales": packed_xT[1],
        "w1": (n((K, N)) / np.sqrt(K) / s).astype(np.float32),
        "val0": (-np.random.uniform(0.0, 3.0, (N, V))).astype(np.float32),
        "offs": striped(np.random.permutation(T)[:S]),
        "dst": striped(np.random.permutation(np.concatenate([np.arange(V), np.random.randint(0, V, S - V)]))),
    }


def reference(x_words, x_scales, w1, val0, offs, dst):
    xq = unpack_weight(x_words, x_scales)[:, unstriped(offs)]
    rew = -1.0 * (np.log(np.exp(mxq(f64(w1), 0, "e4m3").T @ xq) + 1.0))
    qa = rew + f64(val0)[:, unstriped(dst)]
    ea = np.exp(qa)
    va = np.log(ea.reshape(len(ea), -1, D).sum(axis=2))
    qb = rew + va[:, unstriped(dst)]
    eb = np.exp(qb)
    sb = eb.reshape(len(eb), -1, D).sum(axis=2)
    return eb / np.repeat(sb, D, axis=1)

@@ -1,0 +1,155 @@
+from contextlib import ExitStack
+
+import concourse.mybir as mybir
+
+K, T, S, N, V = 512, 2048, 512, 256, 256
+FLOPS = 2 * K * N * S
+
+F32 = mybir.dt.float32
+BF16 = mybir.dt.bfloat16
+I32 = mybir.dt.int32
+U32 = mybir.dt.uint32
+U16 = mybir.dt.uint16
+U8 = mybir.dt.uint8
+FP8X4 = mybir.dt.float8_e4m3fn_x4
+ACT = mybir.ActivationFunctionType
+ALU = mybir.AluOpType
+
+P = 128
+PACK = 4
+BLOCKS = N // P
+HALF = S // 2
+VAL_WINDOW = 2048
+EXP_WINDOW = 704
+NODE_WINDOW = 528
+
+
+def tile_picked_ysoftvi_pol_p_kernel(tc, x_words, x_scales, w1, val0, offs, dst, out):
+    nc = tc.nc
+    with ExitStack() as ctx:
+        pool = ctx.enter_context(tc.tile_pool(name="sb", bufs=1))
+        psum = ctx.enter_context(tc.psum_pool(name="ps", bufs=1))
+
+        offs_t = pool.tile([P, S // 16], U16, name="offs_t")
+        dst_t = pool.tile([P, S // 16], U16, name="dst_t")
+        scale_win = pool.tile([P, T], U8, name="scale_win", align_bytes=64)
+        word_win = pool.tile([P, T], I32, name="word_win", align_bytes=64)
+        val_win = pool.tile([P, VAL_WINDOW], F32, name="val_win")
+        exp_win = pool.tile([P, EXP_WINDOW], F32, name="exp_win")
+        node_win = [pool.tile([P, NODE_WINDOW], F32, name=f"node_win{b}") for b in range(BLOCKS)]
+        w_raw = [pool.tile([P, PACK, P], F32, name=f"w_raw{b}") for b in range(BLOCKS)]
+        warm = pool.tile([P, 8], F32, name="warm")
+
+        nc.vector.memset(scale_win[:].bitcast(I32)[:, :320], 0)
+        nc.gpsimd.memset(scale_win[:].bitcast(I32)[:, 320:], 0)
+        nc.vector.memset(warm[:, 0:1], 0.0)
+        nc.vector.memset(val_win[:, BLOCKS * V : 1280], 0.0)
+        nc.gpsimd.memset(val_win[:, 1280:], 0.0)
+        nc.vector.memset(exp_win[:, V:], 0.0)
+        for b in range(BLOCKS):
+            nc.gpsimd.memset(node_win[b][:, V:], 0.0)
+
+        w_rows = w1.rearrange("(p t) m -> p t m", t=PACK)
+        nc.sync.dma_start(dst_t[:], dst)
+        nc.sync.dma_start(val_win[:, : BLOCKS * V].rearrange("p (b v) -> p b v", b=BLOCKS), val0.rearrange("(b p) v -> p b v", b=BLOCKS))
+        nc.sync.dma_start(offs_t[:], offs)
+        nc.sync.dma_start(w_raw[0][:], w_rows[:, :, :P])
+        for q in range(4):
+            nc.sync.dma_start(scale_win[32 * q : 32 * q + 4, :].bitcast(I32), x_scales[0, 4 * q : 4 * q + 4, :].bitcast(I32))
+        nc.sync.dma_start(word_win[:], x_words[0].rearrange("p n t -> p (n t)").bitcast(I32))
+        nc.sync.dma_start(w_raw[1][:], w_rows[:, :, P:])
+
+        nc.scalar.activation(warm[:, 1:2], warm[:, 0:1], ACT.Exp)
+
+        gain = [pool.tile([P, S], F32, name=f"gain{b}") for b in range(BLOCKS)]
+        nc.scalar.activation(exp_win[:, :V], val_win[:, V : 2 * V], ACT.Exp)
+        nc.scalar.activation(gain[0][:], val_win[:].indirect(dst_t[:]), ACT.Exp)
+        nc.scalar.activation(warm[:, 2:3], gain[0][:, 0:1], ACT.Sigmoid)
+
+        def quantize_weights(b):
+            grouped = pool.tile([P, P, PACK], BF16, name=f"w_grp{b}", align_bytes=64)
+            nc.vector.tensor_copy(
+                grouped[:].rearrange("p (c i) t -> p c t i", i=4),
+                w_raw[b][:].rearrange("p t (c i) -> p c t i", i=4),
+            )
+            codes = pool.tile([P, P], U32, name=f"w_codes{b}", align_bytes=64)
+            scales = pool.tile([P, P], U8, name=f"w_scales{b}", align_bytes=64)
+            nc.vector.quantize_mx(out=codes[:].bitcast(FP8X4), scales=scales[:], in_=grouped[:].rearrange("p c t -> p (c t)"))
+            return codes, scales
+
+        x_bytes = pool.tile([P, S], U8, name="x_bytes", align_bytes=64)
+        nc.vector.tensor_copy(gain[1][:], exp_win[:].indirect(dst_t[:]))
+        weights = [quantize_weights(0)]
+        nc.vector.tensor_copy(x_bytes[:], scale_win[:].indirect(offs_t[:]))
+        x_codes = pool.tile([P, S], U32, name="x_codes", align_bytes=64)
+        for h in range(2):
+            nc.vector.tensor_copy(x_codes[:, h * HALF : (h + 1) * HALF], word_win[:].bitcast(U32).indirect(offs_t[:, 16 * h : 16 * h + 16]))
+        weights.append(quantize_weights(1))
+
+        sig = [pool.tile([P, S], F32, name=f"sig{b}") for b in range(BLOCKS)]
+        ea = [pool.tile([P, S], F32, name=f"ea{b}") for b in range(BLOCKS)]
+
+        def first_round(b, lo, hi):
+            z = psum.tile([P, hi - lo], F32, name=f"z{b}_{lo}")
+            nc.tensor.matmul_mx(
+                z[:],
+                lhsT=weights[b][0][:].bitcast(FP8X4),
+                lhsT_scale=weights[b][1][:],
+                rhs=x_codes[:, lo:hi].bitcast(FP8X4),
+                rhs_scale=x_bytes[:, lo:hi],
+                start=True,
+                stop=True,
+            )
+            nc.scalar.activation(sig[b][:, lo:hi], z[:], ACT.Sigmoid, scale=-1.0)
+
+        def edge_terms(b, lo, hi):
+            nc.vector.tensor_tensor(ea[b][:, lo:hi], sig[b][:, lo:hi], gain[b][:, lo:hi], ALU.mult)
+
+        def node_sums(b, lo, hi):
+            pairs = ea[b][:, lo:hi].rearrange("p (v d) -> p v d", d=2)
+            nc.vector.tensor_tensor(node_win[b][:, lo // 2 : hi // 2], pairs[:, :, 0], pairs[:, :, 1], ALU.add)
+
+        out_rows = out.rearrange("(b p) j -> p b j", b=BLOCKS)
+        pieces = [(0, 0, S), (1, 0, HALF), (1, HALF, S)]
+        eb, inv = {}, {}
+
+        def fetch(i):
+            b, lo, hi = pieces[i]
+            eb[i] = pool.tile([P, hi - lo], F32, name=f"eb{i}")
+            nc.vector.tensor_tensor(eb[i][:], node_win[b][:].indirect(dst_t[:, lo // 16 : hi // 16]), sig[b][:, lo:hi], ALU.mult)
+
+        def norm(i):
+            b, lo, hi = pieces[i]
+            n = (hi - lo) // 2
+            pairs = eb[i][:].rearrange("p (v d) -> p v d", d=2)
+            sb = pool.tile([P, n], F32, name=f"sb{i}", tag="gain1" if i == 0 else f"sb{i}")
+            nc.vector.tensor_tensor(sb[:], pairs[:, :, 0], pairs[:, :, 1], ALU.add)
+            root = pool.tile([P, n], F32, name=f"root{i}")
+            nc.scalar.activation(root[:], sb[:], ACT.Abs_reciprocal_sqrt)
+            inv[i] = pool.tile([P, n], F32, name=f"inv{i}")
+            nc.scalar.activation(inv[i][:], root[:], ACT.Square)
+
+        def finish(i):
+            b, lo, hi = pieces[i]
+            n = (hi - lo) // 2
+            res = pool.tile([P, n, 2], F32, name=f"res{i}")
+            nc.vector.tensor_tensor(res[:], eb[i][:].rearrange("p (v d) -> p v d", d=2), inv[i][:].unsqueeze(2).to_broadcast([P, n, 2]), ALU.mult)
+            nc.sync.dma_start(out_rows[:, b, lo:hi], res[:].rearrange("p v d -> p (v d)"))
+
+        for lo, hi in ((0, HALF), (HALF, S)):
+            first_round(0, lo, hi)
+            edge_terms(0, lo, hi)
+            node_sums(0, lo, hi)
+        first_round(1, 0, S)
+        nc.scalar.activation(warm[:, 3:4], sig[1][:, S - 1 : S], ACT.Abs_reciprocal_sqrt)
+        fetch(0)
+        edge_terms(1, 0, S)
+        norm(0)
+        node_sums(1, 0, S)
+        fetch(1)
+        fetch(2)
+        norm(1)
+        norm(2)
+        finish(0)
+        finish(1)
+        finish(2)

@@ -20,7 +20,7 @@ PACK = 4
 BLOCKS = N // P
 HALF = S // 2
 VAL_WINDOW = 2048
-EXP_WINDOW = 704
+EXP_WINDOW = 272
 NODE_WINDOW = 528
 
 
@@ -37,7 +37,7 @@ def tile_picked_ysoftvi_pol_p_kernel(tc, x_words, x_scales, w1, val0, offs, dst,
         val_win = pool.tile([P, VAL_WINDOW], F32, name="val_win")
         exp_win = pool.tile([P, EXP_WINDOW], F32, name="exp_win")
         node_win = [pool.tile([P, NODE_WINDOW], F32, name=f"node_win{b}") for b in range(BLOCKS)]
-        w_raw = [pool.tile([P, PACK, P], F32, name=f"w_raw{b}") for b in range(BLOCKS)]
+        w_raw = pool.tile([P, PACK, N], F32, name="w_raw")
         warm = pool.tile([P, 8], F32, name="warm")
 
         nc.vector.memset(scale_win[:].bitcast(I32)[:, :320], 0)
@@ -53,38 +53,36 @@ def tile_picked_ysoftvi_pol_p_kernel(tc, x_words, x_scales, w1, val0, offs, dst,
         nc.sync.dma_start(dst_t[:], dst)
         nc.sync.dma_start(val_win[:, : BLOCKS * V].rearrange("p (b v) -> p b v", b=BLOCKS), val0.rearrange("(b p) v -> p b v", b=BLOCKS))
         nc.sync.dma_start(offs_t[:], offs)
-        nc.sync.dma_start(w_raw[0][:], w_rows[:, :, :P])
-        for q in range(4):
-            nc.sync.dma_start(scale_win[32 * q : 32 * q + 4, :].bitcast(I32), x_scales[0, 4 * q : 4 * q + 4, :].bitcast(I32))
+        nc.sync.dma_start(w_raw[:], w_rows)
+        for r in range(4):
+            nc.sync.dma_start(scale_win[r:P:32, :].bitcast(I32), x_scales[0, r:16:4, :].bitcast(I32))
         nc.sync.dma_start(word_win[:], x_words[0].rearrange("p n t -> p (n t)").bitcast(I32))
-        nc.sync.dma_start(w_raw[1][:], w_rows[:, :, P:])
 
         nc.scalar.activation(warm[:, 1:2], warm[:, 0:1], ACT.Exp)
 
-        gain = [pool.tile([P, S], F32, name=f"gain{b}") for b in range(BLOCKS)]
+        gain0 = pool.tile([P, S], F32, name="gain0")
         nc.scalar.activation(exp_win[:, :V], val_win[:, V : 2 * V], ACT.Exp)
-        nc.scalar.activation(gain[0][:], val_win[:].indirect(dst_t[:]), ACT.Exp)
-        nc.scalar.activation(warm[:, 2:3], gain[0][:, 0:1], ACT.Sigmoid)
-
-        def quantize_weights(b):
-            grouped = pool.tile([P, P, PACK], BF16, name=f"w_grp{b}", align_bytes=64)
-            nc.vector.tensor_copy(
-                grouped[:].rearrange("p (c i) t -> p c t i", i=4),
-                w_raw[b][:].rearrange("p t (c i) -> p c t i", i=4),
-            )
-            codes = pool.tile([P, P], U32, name=f"w_codes{b}", align_bytes=64)
-            scales = pool.tile([P, P], U8, name=f"w_scales{b}", align_bytes=64)
-            nc.vector.quantize_mx(out=codes[:].bitcast(FP8X4), scales=scales[:], in_=grouped[:].rearrange("p c t -> p (c t)"))
-            return codes, scales
+        nc.scalar.activation(gain0[:], val_win[:].indirect(dst_t[:]), ACT.Exp)
 
         x_bytes = pool.tile([P, S], U8, name="x_bytes", align_bytes=64)
-        nc.vector.tensor_copy(gain[1][:], exp_win[:].indirect(dst_t[:]))
-        weights = [quantize_weights(0)]
+        gain1a = pool.tile([P, HALF], F32, name="gain1a")
+        nc.vector.tensor_copy(gain1a[:], exp_win[:].indirect(dst_t[:, :16]))
+        w_grp = pool.tile([P, N, PACK], BF16, name="w_grp", align_bytes=64)
+        nc.vector.tensor_copy(
+            w_grp[:].rearrange("p (c i) t -> p c t i", i=4),
+            w_raw[:].rearrange("p t (c i) -> p c t i", i=4),
+        )
+        w_codes = pool.tile([P, N], U32, name="w_codes", align_bytes=64)
+        w_scales = pool.tile([P, N], U8, name="w_scales", align_bytes=64)
+        nc.vector.quantize_mx(out=w_codes[:].bitcast(FP8X4), scales=w_scales[:], in_=w_grp[:].rearrange("p c t -> p (c t)"))
+        nc.scalar.activation(warm[:, 2:3], gain0[:, 0:1], ACT.Sigmoid)
         nc.vector.tensor_copy(x_bytes[:], scale_win[:].indirect(offs_t[:]))
         x_codes = pool.tile([P, S], U32, name="x_codes", align_bytes=64)
         for h in range(2):
             nc.vector.tensor_copy(x_codes[:, h * HALF : (h + 1) * HALF], word_win[:].bitcast(U32).indirect(offs_t[:, 16 * h : 16 * h + 16]))
-        weights.append(quantize_weights(1))
+        gain1b = pool.tile([P, HALF], F32, name="gain1b", tag="word_win", align_bytes=64)
+        nc.vector.tensor_copy(gain1b[:], exp_win[:].indirect(dst_t[:, 16:]))
+        gain = {(0, 0): gain0[:, :HALF], (0, HALF): gain0[:, HALF:], (1, 0): gain1a[:], (1, HALF): gain1b[:]}
 
         sig = [pool.tile([P, S], F32, name=f"sig{b}") for b in range(BLOCKS)]
         ea = [pool.tile([P, S], F32, name=f"ea{b}") for b in range(BLOCKS)]
@@ -93,8 +91,8 @@ def tile_picked_ysoftvi_pol_p_kernel(tc, x_words, x_scales, w1, val0, offs, dst,
             z = psum.tile([P, hi - lo], F32, name=f"z{b}_{lo}")
             nc.tensor.matmul_mx(
                 z[:],
-                lhsT=weights[b][0][:].bitcast(FP8X4),
-                lhsT_scale=weights[b][1][:],
+                lhsT=w_codes[:, b * P : (b + 1) * P].bitcast(FP8X4),
+                lhsT_scale=w_scales[:, b * P : (b + 1) * P],
                 rhs=x_codes[:, lo:hi].bitcast(FP8X4),
                 rhs_scale=x_bytes[:, lo:hi],
                 start=True,
@@ -103,7 +101,7 @@ def tile_picked_ysoftvi_pol_p_kernel(tc, x_words, x_scales, w1, val0, offs, dst,
             nc.scalar.activation(sig[b][:, lo:hi], z[:], ACT.Sigmoid, scale=-1.0)
 
         def edge_terms(b, lo, hi):
-            nc.vector.tensor_tensor(ea[b][:, lo:hi], sig[b][:, lo:hi], gain[b][:, lo:hi], ALU.mult)
+            nc.vector.tensor_tensor(ea[b][:, lo:hi], sig[b][:, lo:hi], gain[b, lo], ALU.mult)
 
         def node_sums(b, lo, hi):
             pairs = ea[b][:, lo:hi].rearrange("p (v d) -> p v d", d=2)
@@ -115,14 +113,14 @@ def tile_picked_ysoftvi_pol_p_kernel(tc, x_words, x_scales, w1, val0, offs, dst,
 
         def fetch(i):
             b, lo, hi = pieces[i]
-            eb[i] = pool.tile([P, hi - lo], F32, name=f"eb{i}")
+            eb[i] = pool.tile([P, hi - lo], F32, name=f"eb{i}", tag="gain1a" if i == 0 else f"eb{i}")
             nc.vector.tensor_tensor(eb[i][:], node_win[b][:].indirect(dst_t[:, lo // 16 : hi // 16]), sig[b][:, lo:hi], ALU.mult)
 
         def norm(i):
             b, lo, hi = pieces[i]
             n = (hi - lo) // 2
             pairs = eb[i][:].rearrange("p (v d) -> p v d", d=2)
-            sb = pool.tile([P, n], F32, name=f"sb{i}", tag="gain1" if i == 0 else f"sb{i}")
+            sb = pool.tile([P, n], F32, name=f"sb{i}")
             nc.vector.tensor_tensor(sb[:], pairs[:, :, 0], pairs[:, :, 1], ALU.add)
             root = pool.tile([P, n], F32, name=f"root{i}")
             nc.scalar.activation(root[:], sb[:], ACT.Abs_reciprocal_sqrt)
@@ -136,16 +134,21 @@ def tile_picked_ysoftvi_pol_p_kernel(tc, x_words, x_scales, w1, val0, offs, dst,
             nc.vector.tensor_tensor(res[:], eb[i][:].rearrange("p (v d) -> p v d", d=2), inv[i][:].unsqueeze(2).to_broadcast([P, n, 2]), ALU.mult)
             nc.sync.dma_start(out_rows[:, b, lo:hi], res[:].rearrange("p v d -> p (v d)"))
 
-        for lo, hi in ((0, HALF), (HALF, S)):
-            first_round(0, lo, hi)
-            edge_terms(0, lo, hi)
-            node_sums(0, lo, hi)
-        first_round(1, 0, S)
+        halves = ((0, HALF), (HALF, S))
+        for lo, hi in halves:
+            for b in range(BLOCKS):
+                first_round(b, lo, hi)
         nc.scalar.activation(warm[:, 3:4], sig[1][:, S - 1 : S], ACT.Abs_reciprocal_sqrt)
+        edge_terms(0, 0, HALF)
+        edge_terms(1, 0, HALF)
+        node_sums(0, 0, HALF)
+        edge_terms(0, HALF, S)
+        edge_terms(1, HALF, S)
+        node_sums(0, HALF, S)
+        node_sums(1, 0, HALF)
         fetch(0)
-        edge_terms(1, 0, S)
+        node_sums(1, HALF, S)
         norm(0)
-        node_sums(1, 0, S)
         fetch(1)
         fetch(2)
         norm(1)

from contextlib import ExitStack

import concourse.mybir as mybir

K, T, S, N, V = 512, 2048, 512, 256, 256
FLOPS = 2 * K * N * S

F32 = mybir.dt.float32
BF16 = mybir.dt.bfloat16
I32 = mybir.dt.int32
U32 = mybir.dt.uint32
U16 = mybir.dt.uint16
U8 = mybir.dt.uint8
FP8X4 = mybir.dt.float8_e4m3fn_x4
ACT = mybir.ActivationFunctionType
ALU = mybir.AluOpType

P = 128
PACK = 4
BLOCKS = N // P
HALF = S // 2
VAL_WINDOW = 2048
EXP_WINDOW = 272
NODE_WINDOW = 528


def tile_picked_ysoftvi_pol_p_kernel(tc, x_words, x_scales, w1, val0, offs, dst, out):
    nc = tc.nc
    with ExitStack() as ctx:
        pool = ctx.enter_context(tc.tile_pool(name="sb", bufs=1))
        psum = ctx.enter_context(tc.psum_pool(name="ps", bufs=1))

        offs_t = pool.tile([P, S // 16], U16, name="offs_t")
        dst_t = pool.tile([P, S // 16], U16, name="dst_t")
        scale_win = pool.tile([P, T], U8, name="scale_win", align_bytes=64)
        word_win = pool.tile([P, T], I32, name="word_win", align_bytes=64)
        val_win = pool.tile([P, VAL_WINDOW], F32, name="val_win")
        exp_win = pool.tile([P, EXP_WINDOW], F32, name="exp_win")
        node_win = [pool.tile([P, NODE_WINDOW], F32, name=f"node_win{b}") for b in range(BLOCKS)]
        w_raw = pool.tile([P, PACK, N], F32, name="w_raw")
        warm = pool.tile([P, 8], F32, name="warm")

        nc.vector.memset(scale_win[:].bitcast(I32)[:, :320], 0)
        nc.gpsimd.memset(scale_win[:].bitcast(I32)[:, 320:], 0)
        nc.vector.memset(warm[:, 0:1], 0.0)
        nc.vector.memset(val_win[:, BLOCKS * V : 1280], 0.0)
        nc.gpsimd.memset(val_win[:, 1280:], 0.0)
        nc.vector.memset(exp_win[:, V:], 0.0)
        for b in range(BLOCKS):
            nc.gpsimd.memset(node_win[b][:, V:], 0.0)

        w_rows = w1.rearrange("(p t) m -> p t m", t=PACK)
        nc.sync.dma_start(dst_t[:], dst)
        nc.sync.dma_start(val_win[:, : BLOCKS * V].rearrange("p (b v) -> p b v", b=BLOCKS), val0.rearrange("(b p) v -> p b v", b=BLOCKS))
        nc.sync.dma_start(offs_t[:], offs)
        nc.sync.dma_start(w_raw[:], w_rows)
        for r in range(4):
            nc.sync.dma_start(scale_win[r:P:32, :].bitcast(I32), x_scales[0, r:16:4, :].bitcast(I32))
        nc.sync.dma_start(word_win[:], x_words[0].rearrange("p n t -> p (n t)").bitcast(I32))

        nc.scalar.activation(warm[:, 1:2], warm[:, 0:1], ACT.Exp)

        gain0 = pool.tile([P, S], F32, name="gain0")
        nc.scalar.activation(exp_win[:, :V], val_win[:, V : 2 * V], ACT.Exp)
        nc.scalar.activation(gain0[:], val_win[:].indirect(dst_t[:]), ACT.Exp)

        x_bytes = pool.tile([P, S], U8, name="x_bytes", align_bytes=64)
        gain1a = pool.tile([P, HALF], F32, name="gain1a")
        nc.vector.tensor_copy(gain1a[:], exp_win[:].indirect(dst_t[:, :16]))
        w_grp = pool.tile([P, N, PACK], BF16, name="w_grp", align_bytes=64)
        nc.vector.tensor_copy(
            w_grp[:].rearrange("p (c i) t -> p c t i", i=4),
            w_raw[:].rearrange("p t (c i) -> p c t i", i=4),
        )
        w_codes = pool.tile([P, N], U32, name="w_codes", align_bytes=64)
        w_scales = pool.tile([P, N], U8, name="w_scales", align_bytes=64)
        nc.vector.quantize_mx(out=w_codes[:].bitcast(FP8X4), scales=w_scales[:], in_=w_grp[:].rearrange("p c t -> p (c t)"))
        nc.scalar.activation(warm[:, 2:3], gain0[:, 0:1], ACT.Sigmoid)
        nc.vector.tensor_copy(x_bytes[:], scale_win[:].indirect(offs_t[:]))
        x_codes = pool.tile([P, S], U32, name="x_codes", align_bytes=64)
        for h in range(2):
            nc.vector.tensor_copy(x_codes[:, h * HALF : (h + 1) * HALF], word_win[:].bitcast(U32).indirect(offs_t[:, 16 * h : 16 * h + 16]))
        gain1b = pool.tile([P, HALF], F32, name="gain1b", tag="word_win", align_bytes=64)
        nc.vector.tensor_copy(gain1b[:], exp_win[:].indirect(dst_t[:, 16:]))
        gain = {(0, 0): gain0[:, :HALF], (0, HALF): gain0[:, HALF:], (1, 0): gain1a[:], (1, HALF): gain1b[:]}

        sig = [pool.tile([P, S], F32, name=f"sig{b}") for b in range(BLOCKS)]
        ea = [pool.tile([P, S], F32, name=f"ea{b}") for b in range(BLOCKS)]

        def first_round(b, lo, hi):
            z = psum.tile([P, hi - lo], F32, name=f"z{b}_{lo}")
            nc.tensor.matmul_mx(
                z[:],
                lhsT=w_codes[:, b * P : (b + 1) * P].bitcast(FP8X4),
                lhsT_scale=w_scales[:, b * P : (b + 1) * P],
                rhs=x_codes[:, lo:hi].bitcast(FP8X4),
                rhs_scale=x_bytes[:, lo:hi],
                start=True,
                stop=True,
            )
            nc.scalar.activation(sig[b][:, lo:hi], z[:], ACT.Sigmoid, scale=-1.0)

        def edge_terms(b, lo, hi):
            nc.vector.tensor_tensor(ea[b][:, lo:hi], sig[b][:, lo:hi], gain[b, lo], ALU.mult)

        def node_sums(b, lo, hi):
            pairs = ea[b][:, lo:hi].rearrange("p (v d) -> p v d", d=2)
            nc.vector.tensor_tensor(node_win[b][:, lo // 2 : hi // 2], pairs[:, :, 0], pairs[:, :, 1], ALU.add)

        out_rows = out.rearrange("(b p) j -> p b j", b=BLOCKS)
        pieces = [(0, 0, S), (1, 0, HALF), (1, HALF, S)]
        eb, inv = {}, {}

        def fetch(i):
            b, lo, hi = pieces[i]
            eb[i] = pool.tile([P, hi - lo], F32, name=f"eb{i}", tag="gain1a" if i == 0 else f"eb{i}")
            nc.vector.tensor_tensor(eb[i][:], node_win[b][:].indirect(dst_t[:, lo // 16 : hi // 16]), sig[b][:, lo:hi], ALU.mult)

        def norm(i):
            b, lo, hi = pieces[i]
            n = (hi - lo) // 2
            pairs = eb[i][:].rearrange("p (v d) -> p v d", d=2)
            sb = pool.tile([P, n], F32, name=f"sb{i}")
            nc.vector.tensor_tensor(sb[:], pairs[:, :, 0], pairs[:, :, 1], ALU.add)
            root = pool.tile([P, n], F32, name=f"root{i}")
            nc.scalar.activation(root[:], sb[:], ACT.Abs_reciprocal_sqrt)
            inv[i] = pool.tile([P, n], F32, name=f"inv{i}")
            nc.scalar.activation(inv[i][:], root[:], ACT.Square)

        def finish(i):
            b, lo, hi = pieces[i]
            n = (hi - lo) // 2
            res = pool.tile([P, n, 2], F32, name=f"res{i}")
            nc.vector.tensor_tensor(res[:], eb[i][:].rearrange("p (v d) -> p v d", d=2), inv[i][:].unsqueeze(2).to_broadcast([P, n, 2]), ALU.mult)
            nc.sync.dma_start(out_rows[:, b, lo:hi], res[:].rearrange("p v d -> p (v d)"))

        halves = ((0, HALF), (HALF, S))
        for lo, hi in halves:
            for b in range(BLOCKS):
                first_round(b, lo, hi)
        nc.scalar.activation(warm[:, 3:4], sig[1][:, S - 1 : S], ACT.Abs_reciprocal_sqrt)
        edge_terms(0, 0, HALF)
        edge_terms(1, 0, HALF)
        node_sums(0, 0, HALF)
        edge_terms(0, HALF, S)
        edge_terms(1, HALF, S)
        node_sums(0, HALF, S)
        node_sums(1, 0, HALF)
        fetch(0)
        node_sums(1, HALF, S)
        norm(0)
        fetch(1)
        fetch(2)
        norm(1)
        norm(2)
        finish(0)
        finish(1)
        finish(2)
